import numpy as np
import ml_dtypes


def mxq(x, axis, fmt="e4m3"):
    dtype, down = {"e4m3": (ml_dtypes.float8_e4m3fn, 7), "e5m2": (ml_dtypes.float8_e5m2, 14)}[fmt]
    v = np.moveaxis(np.asarray(x, np.float32).astype(ml_dtypes.bfloat16).astype(np.float64), axis, -1)
    blocks = v.reshape(v.shape[:-1] + (-1, 32))
    amax = np.abs(blocks).max(-1, keepdims=True)
    byte = np.maximum(np.where(amax > 0, np.frexp(amax)[1] - 1 + 127, 0) - down, 1)
    scale = np.exp2(byte - 127.0)
    codes = (blocks / scale).astype(np.float32).astype(dtype).astype(np.float64)
    return np.moveaxis((codes * scale).reshape(v.shape), -1, axis)


WIDE = False


def mx_kscale(k):
    if not WIDE:
        return np.ones(k)
    levels = np.array([10, -10, 5, -5, 0])
    if k % 512:
        return np.exp2(np.random.permutation(np.resize(levels, k // 32))).repeat(32)
    a = np.empty((k // 512, 16))
    for p in range(k // 512):
        a[p, :8] = np.random.permutation(np.resize(levels, 8))
        for g in range(8):
            far = levels[np.abs(levels - a[p, g]) >= 10]
            a[p, g + 8] = far[np.random.randint(len(far))]
    return np.exp2(a.ravel()).repeat(32)


def f64(x):
    return np.asarray(x).astype(np.float64)


def striped(idx):
    return np.tile(np.asarray(idx).reshape(-1, 16).T, (8, 1)).astype(np.uint16)


def unstriped(offs):
    return offs[:16].T.reshape(-1).astype(np.int64)


E2M1 = np.array([0.0, 0.5, 1.0, 1.5, 2.0, 3.0, 4.0, 6.0, -0.0, -0.5, -1.0, -1.5, -2.0, -3.0, -4.0, -6.0])


def pack_weight(w, fmt):
    k, n = w.shape
    w = f64(np.asarray(w, np.float32).astype(ml_dtypes.bfloat16)).reshape(k // 32, 32, n)
    amax = np.abs(w).max(1)
    if fmt == "e4m3":
        byte = np.frexp(amax)[1] - 1 + 127 - 7
    else:
        mant, ex = np.frexp(amax / 6.0)
        byte = np.where(mant > 0.5, ex, ex - 1) + 127
    byte = np.clip(np.where(amax > 0, byte, 1), 1, 254)
    scaled = (w * np.exp2(127.0 - byte)[:, None, :]).reshape(k, n).astype(np.float32)
    by_word = np.ascontiguousarray(scaled.reshape(k // 512, 128, 4, n).transpose(0, 1, 3, 2))
    if fmt == "e4m3":
        words = by_word.astype(ml_dtypes.float8_e4m3fn).view(np.uint8)
    else:
        c = by_word.astype(ml_dtypes.float4_e2m1fn).view(np.uint8) & 0xF
        words = (c[..., 0::2] | (c[..., 1::2] << 4)).reshape(k // 512, 128, 2 * n)
    return np.ascontiguousarray(words), np.ascontiguousarray(byte.astype(np.uint8).reshape(k // 512, 16, n))


def unpack_weight(words, scales, fmt):
    g, _, n = scales.shape
    words = np.ascontiguousarray(words).reshape(g, 128, n, -1)
    if fmt == "e4m3":
        vals = words.view(ml_dtypes.float8_e4m3fn).astype(np.float64)
    else:
        nib = np.empty((g, 128, n, 4), np.uint8)
        nib[..., 0::2] = words & 0xF
        nib[..., 1::2] = words >> 4
        vals = E2M1[nib]
    vals = vals * np.repeat(np.exp2(scales.astype(np.float64) - 127.0), 8, axis=1)[..., None]
    return vals.transpose(0, 1, 3, 2).reshape(g * 512, n)


D, K, T, I, Q = 512, 512, 2048, 512, 256


def setup_inputs():
    n = np.random.standard_normal
    idx = np.random.permutation(T)[:I]
    fd = mx_kscale(D)
    candp = pack_weight(n((D, T)) / fd[:, None], "e4m3")
    return {
        "cand_words": candp[0],
        "cand_scales": candp[1],
        "theta": (n((D, Q)) * 1 / np.sqrt(D) * fd[:, None]).astype(np.float32),
        "inv": (n((D, K)) * 1.5 / np.sqrt(D) * fd[:, None]).astype(np.float32),
        "crow": (n((K, T))).astype(np.float32),
        "bold": (np.random.uniform(1.0, 3.0, (1, Q))).astype(np.float32),
        "offs": striped(idx),
    }


def reference(cand_words, cand_scales, theta, inv, crow, bold, offs):
    idx = unstriped(offs)
    candu = unpack_weight(cand_words, cand_scales, "e4m3")
    candidxg = candu[:, idx]
    thetaq = mxq(f64(theta), 0, "e4m3")
    a = candidxg.T @ thetaq
    invq = mxq(f64(inv), 0, "e4m3")
    z = candidxg.T @ invq
    cr = f64(crow)[:, idx].T
    qf = np.sqrt(np.abs(np.sum(z * cr, axis=1, keepdims=True)) / 512.0 + 0.01)
    y = a + qf * f64(bold)
    return y

@@ -1,0 +1,171 @@
+from contextlib import ExitStack
+
+import concourse.mybir as mybir
+from concourse.masks import make_identity
+
+D, K, T, I, Q = 512, 512, 2048, 512, 256
+FLOPS = 2 * D * I * (Q + K)
+
+F32 = mybir.dt.float32
+BF16 = mybir.dt.bfloat16
+I32 = mybir.dt.int32
+U32 = mybir.dt.uint32
+U16 = mybir.dt.uint16
+U8 = mybir.dt.uint8
+FP8X4 = mybir.dt.float8_e4m3fn_x4
+ALU = mybir.AluOpType
+ACT = mybir.ActivationFunctionType
+
+P = 128
+PACK = 4
+K_TILES = K // P
+I_TILES = I // P
+OFFS_COLS = P // 16
+
+
+def tile_attend_confidencebounds_kernel(tc, cand_words, cand_scales, theta, inv, crow, bold, offs, out):
+    nc = tc.nc
+    with ExitStack() as ctx:
+        keep = ctx.enter_context(tc.tile_pool(name="keep", bufs=1))
+        psum = ctx.enter_context(tc.psum_pool(name="psum", bufs=1))
+        zpsum = ctx.enter_context(tc.psum_pool(name="zpsum", bufs=2))
+
+        offsets = keep.tile([P, I // 16], U16, name="offsets")
+        inv_raw = keep.tile([P, PACK, K], F32, name="inv_raw")
+        words = keep.tile([P, T], U32, name="words", align_bytes=64)
+        scales = keep.tile([P, T], U8, name="scales", align_bytes=64)
+        theta_raw = keep.tile([P, PACK, Q], F32, name="theta_raw")
+        crow_sb = [keep.tile([P, T], F32, name="crow%d" % j) for j in range(K_TILES)]
+        bold_col = keep.tile([P, 2], F32, name="bold_col")
+
+        nc.sync.dma_start(offsets[:], offs)
+        nc.sync.dma_start(out=inv_raw[:], in_=inv.rearrange("(p j) w -> p j w", j=PACK))
+        nc.sync.dma_start(out=words[:].bitcast(I32), in_=cand_words[0].rearrange("p n t -> p (n t)").bitcast(I32))
+        nc.sync.dma_start(out=crow_sb[0][:], in_=crow[0:P, :])
+        nc.sync.dma_start(out=theta_raw[:], in_=theta.rearrange("(p j) w -> p j w", j=PACK))
+        for j in range(1, K_TILES):
+            nc.sync.dma_start(out=crow_sb[j][:], in_=crow[j * P : (j + 1) * P, :])
+
+        nc.vector.memset(scales[:].bitcast(I32), 0)
+        for g in range(4):
+            nc.scalar.dma_start(
+                out=scales[32 * g : 32 * g + 4, :].bitcast(I32),
+                in_=cand_scales[0, 4 * g : 4 * g + 4, :].bitcast(I32),
+            )
+        nc.scalar.dma_start(out=bold_col[:], in_=bold[0].rearrange("(p c) -> p c", c=2))
+
+        ident = keep.tile([P, P], F32, name="ident")
+        make_identity(nc, ident[:])
+        warm = keep.tile([P, 1], F32, name="warm")
+        nc.scalar.activation(out=warm[:], in_=ident[:, 0:1], func=ACT.Sqrt, bias=1.0)
+
+        cand_s = keep.tile([P, I], U8, name="cand_s", align_bytes=64)
+        nc.vector.tensor_copy(cand_s[:], scales[:].indirect(offsets[:]))
+
+        def interleave(copy, raw, width, name):
+            grouped = keep.tile([P, width, PACK], BF16, name=name, align_bytes=64)
+            copy(
+                out=grouped[:].rearrange("p (c i) t -> p c t i", i=4),
+                in_=raw[:].rearrange("p t (c i) -> p c t i", i=4),
+            )
+            return grouped
+
+        def quantize(grouped, width, name):
+            codes = keep.tile([P, width], U32, name=name + "_codes", align_bytes=64)
+            plane = keep.tile([P, width], U8, name=name + "_scales", align_bytes=64)
+            nc.vector.quantize_mx(
+                out=codes[:].bitcast(FP8X4), scales=plane[:], in_=grouped[:].rearrange("p w t -> p (w t)")
+            )
+            return codes, plane
+
+        inv_bf = interleave(nc.vector.tensor_copy, inv_raw, K, "inv_bf")
+        inv_q, inv_s = quantize(inv_bf, K, "inv")
+
+        cand_q = keep.tile([P, I], U32, name="cand_q", align_bytes=64)
+        nc.vector.tensor_copy(cand_q[:], words[:].indirect(offsets[:]))
+
+        bold_ps = zpsum.tile([P, 2, P], F32, name="bold_ps", tag="z")
+        for c in range(2):
+            nc.tensor.transpose(bold_ps[:, c, :], bold_col[:, c : c + 1].to_broadcast([P, P]), ident[:])
+        bold_row = keep.tile([P, Q], F32, name="bold_row")
+        nc.scalar.copy(out=bold_row[:].rearrange("p (n c) -> p n c", c=2), in_=bold_ps[:].rearrange("p c n -> p n c"))
+
+        z_sb = []
+        for j in range(K_TILES):
+            cols = slice(j * P, (j + 1) * P)
+            z_ps = zpsum.tile([P, I], F32, name="z_ps%d" % j, tag="z")
+            nc.tensor.matmul_mx(
+                out=z_ps[:],
+                lhsT=inv_q[:, cols].bitcast(FP8X4),
+                lhsT_scale=inv_s[:, cols],
+                rhs=cand_q[:].bitcast(FP8X4),
+                rhs_scale=cand_s[:],
+                start=True,
+                stop=True,
+            )
+            z_tile = keep.tile([P, I], F32, name="z_sb%d" % j)
+            nc.scalar.copy(out=z_tile[:], in_=z_ps[:])
+            z_sb.append(z_tile)
+
+        theta_bf = interleave(nc.scalar.copy, theta_raw, Q, "theta_bf")
+        theta_q, theta_s = quantize(theta_bf, Q, "theta")
+
+        gain = [psum.tile([P, 2, Q], F32, name="gain%d" % h) for h in range(I_TILES // 2)]
+        form = [psum.tile([P, P], F32, name="form%d" % t) for t in range(I_TILES)]
+
+        def gather_times_z(j, t0, t1):
+            prod = keep.tile([P, (t1 - t0) * P], F32, name="prod%d_%d" % (j, t0))
+            nc.vector.tensor_tensor(
+                prod[:],
+                crow_sb[j][:].indirect(offsets[:, t0 * OFFS_COLS : t1 * OFFS_COLS]),
+                z_sb[j][:, t0 * P : t1 * P],
+                ALU.mult,
+            )
+            for t in range(t0, t1):
+                nc.tensor.matmul(
+                    form[t][:],
+                    lhsT=prod[:, (t - t0) * P : (t - t0 + 1) * P],
+                    rhs=ident[:],
+                    is_transpose=True,
+                    start=(j == 0),
+                    stop=(j == K_TILES - 1),
+                )
+
+        gather_times_z(0, 0, I_TILES)
+        for t in range(I_TILES):
+            cols = slice(t * P, (t + 1) * P)
+            nc.tensor.matmul_mx(
+                out=gain[t // 2][:, t % 2, :],
+                lhsT=cand_q[:, cols].bitcast(FP8X4),
+                lhsT_scale=cand_s[:, cols],
+                rhs=theta_q[:].bitcast(FP8X4),
+                rhs_scale=theta_s[:],
+                start=True,
+                stop=True,
+            )
+        for j in range(1, K_TILES - 1):
+            gather_times_z(j, 0, I_TILES)
+
+        widths = []
+        for t in range(I_TILES):
+            gather_times_z(K_TILES - 1, t, t + 1)
+            spill = keep.tile([P, P], F32, name="spill%d" % t)
+            total = keep.tile([P, 1], F32, name="total%d" % t)
+            nc.scalar.activation(out=spill[:], in_=form[t][:], func=ACT.Copy, accum_out=total[:])
+            size = keep.tile([P, 1], F32, name="size%d" % t)
+            nc.scalar.activation(out=size[:], in_=total[:], func=ACT.Abs)
+            width = keep.tile([P, 1], F32, name="width%d" % t)
+            nc.scalar.activation(out=width[:], in_=size[:], func=ACT.Sqrt, scale=1.0 / K, bias=0.01)
+            widths.append(width)
+
+        for t in range(I_TILES):
+            res = keep.tile([P, Q], F32, name="res%d" % t)
+            nc.vector.scalar_tensor_tensor(
+                out=res[:],
+                in0=bold_row[:],
+                scalar=widths[t][:],
+                in1=gain[t // 2][:, t % 2, :],
+                op0=ALU.mult,
+                op1=ALU.add,
+            )
+            nc.sync.dma_start(out=out[t * P : (t + 1) * P, :], in_=res[:])

@@ -38,26 +38,29 @@ def tile_attend_confidencebounds_kernel(tc, cand_words, cand_scales, theta, inv,
         crow_sb = [keep.tile([P, T], F32, name="crow%d" % j) for j in range(K_TILES)]
         bold_col = keep.tile([P, 2], F32, name="bold_col")
 
+        scale_words = scales[:].bitcast(I32)
+        nc.vector.memset(scale_words[:, 0:320], 0)
+        nc.gpsimd.memset(scale_words[:, 320:], 0)
         nc.sync.dma_start(offsets[:], offs)
         nc.sync.dma_start(out=inv_raw[:], in_=inv.rearrange("(p j) w -> p j w", j=PACK))
+        nc.sync.dma_start(out=bold_col[:], in_=bold[0].rearrange("(p c) -> p c", c=2))
+        for g in range(4):
+            nc.sync.dma_start(
+                out=scales[32 * g : 32 * g + 4, :].bitcast(I32),
+                in_=cand_scales[0, 4 * g : 4 * g + 4, :].bitcast(I32),
+            )
         nc.sync.dma_start(out=words[:].bitcast(I32), in_=cand_words[0].rearrange("p n t -> p (n t)").bitcast(I32))
         nc.sync.dma_start(out=crow_sb[0][:], in_=crow[0:P, :])
         nc.sync.dma_start(out=theta_raw[:], in_=theta.rearrange("(p j) w -> p j w", j=PACK))
         for j in range(1, K_TILES):
             nc.sync.dma_start(out=crow_sb[j][:], in_=crow[j * P : (j + 1) * P, :])
 
-        nc.vector.memset(scales[:].bitcast(I32), 0)
-        for g in range(4):
-            nc.scalar.dma_start(
-                out=scales[32 * g : 32 * g + 4, :].bitcast(I32),
-                in_=cand_scales[0, 4 * g : 4 * g + 4, :].bitcast(I32),
-            )
-        nc.scalar.dma_start(out=bold_col[:], in_=bold[0].rearrange("(p c) -> p c", c=2))
-
         ident = keep.tile([P, P], F32, name="ident")
         make_identity(nc, ident[:])
         warm = keep.tile([P, 1], F32, name="warm")
-        nc.scalar.activation(out=warm[:], in_=ident[:, 0:1], func=ACT.Sqrt, bias=1.0)
+        one = keep.tile([P, 1], F32, name="one")
+        nc.vector.memset(one[:], 1.0)
+        nc.scalar.activation(out=warm[:], in_=one[:], func=ACT.Sqrt)
 
         cand_s = keep.tile([P, I], U8, name="cand_s", align_bytes=64)
         nc.vector.tensor_copy(cand_s[:], scales[:].indirect(offsets[:]))

@@ -51,9 +51,9 @@ def tile_attend_confidencebounds_kernel(tc, cand_words, cand_scales, theta, inv,
             )
         nc.sync.dma_start(out=words[:].bitcast(I32), in_=cand_words[0].rearrange("p n t -> p (n t)").bitcast(I32))
         nc.sync.dma_start(out=crow_sb[0][:], in_=crow[0:P, :])
-        nc.sync.dma_start(out=theta_raw[:], in_=theta.rearrange("(p j) w -> p j w", j=PACK))
         for j in range(1, K_TILES):
             nc.sync.dma_start(out=crow_sb[j][:], in_=crow[j * P : (j + 1) * P, :])
+        nc.sync.dma_start(out=theta_raw[:], in_=theta.rearrange("(p j) w -> p j w", j=PACK))
 
         ident = keep.tile([P, P], F32, name="ident")
         make_identity(nc, ident[:])
@@ -69,7 +69,7 @@ def tile_attend_confidencebounds_kernel(tc, cand_words, cand_scales, theta, inv,
             grouped = keep.tile([P, width, PACK], BF16, name=name, align_bytes=64)
             copy(
                 out=grouped[:].rearrange("p (c i) t -> p c t i", i=4),
-                in_=raw[:].rearrange("p t (c i) -> p c t i", i=4),
+                in_=raw.rearrange("p t (c i) -> p c t i", i=4),
             )
             return grouped
 
@@ -81,7 +81,7 @@ def tile_attend_confidencebounds_kernel(tc, cand_words, cand_scales, theta, inv,
             )
             return codes, plane
 
-        inv_bf = interleave(nc.vector.tensor_copy, inv_raw, K, "inv_bf")
+        inv_bf = interleave(nc.vector.tensor_copy, inv_raw[:], K, "inv_bf")
         inv_q, inv_s = quantize(inv_bf, K, "inv")
 
         cand_q = keep.tile([P, I], U32, name="cand_q", align_bytes=64)
@@ -110,10 +110,6 @@ def tile_attend_confidencebounds_kernel(tc, cand_words, cand_scales, theta, inv,
             nc.scalar.copy(out=z_tile[:], in_=z_ps[:])
             z_sb.append(z_tile)
 
-        theta_bf = interleave(nc.scalar.copy, theta_raw, Q, "theta_bf")
-        theta_q, theta_s = quantize(theta_bf, Q, "theta")
-
-        gain = [psum.tile([P, 2, Q], F32, name="gain%d" % h) for h in range(I_TILES // 2)]
         form = [psum.tile([P, P], F32, name="form%d" % t) for t in range(I_TILES)]
 
         def gather_times_z(j, t0, t1):
@@ -134,40 +130,46 @@ def tile_attend_confidencebounds_kernel(tc, cand_words, cand_scales, theta, inv,
                     stop=(j == K_TILES - 1),
                 )
 
-        gather_times_z(0, 0, I_TILES)
-        for t in range(I_TILES):
-            cols = slice(t * P, (t + 1) * P)
-            nc.tensor.matmul_mx(
-                out=gain[t // 2][:, t % 2, :],
-                lhsT=cand_q[:, cols].bitcast(FP8X4),
-                lhsT_scale=cand_s[:, cols],
-                rhs=theta_q[:].bitcast(FP8X4),
-                rhs_scale=theta_s[:],
-                start=True,
-                stop=True,
-            )
-        for j in range(1, K_TILES - 1):
+        for j in range(K_TILES - 1):
             gather_times_z(j, 0, I_TILES)
 
         widths = []
-        for t in range(I_TILES):
-            gather_times_z(K_TILES - 1, t, t + 1)
-            spill = keep.tile([P, P], F32, name="spill%d" % t)
-            total = keep.tile([P, 1], F32, name="total%d" % t)
-            nc.scalar.activation(out=spill[:], in_=form[t][:], func=ACT.Copy, accum_out=total[:])
-            size = keep.tile([P, 1], F32, name="size%d" % t)
+        for pair in range(I_TILES // 2):
+            gather_times_z(K_TILES - 1, 2 * pair, 2 * pair + 2)
+            total = keep.tile([P, 2], F32, name="total%d" % pair)
+            for u in range(2):
+                spill = keep.tile([P, P], F32, name="spill%d_%d" % (pair, u))
+                nc.scalar.activation(out=spill[:], in_=form[2 * pair + u][:], func=ACT.Copy, accum_out=total[:, u : u + 1])
+            size = keep.tile([P, 2], F32, name="size%d" % pair)
             nc.scalar.activation(out=size[:], in_=total[:], func=ACT.Abs)
-            width = keep.tile([P, 1], F32, name="width%d" % t)
+            width = keep.tile([P, 2], F32, name="width%d" % pair)
             nc.scalar.activation(out=width[:], in_=size[:], func=ACT.Sqrt, scale=1.0 / K, bias=0.01)
-            widths.append(width)
+            widths.extend([width[:, 0:1], width[:, 1:2]])
+
+        halves = [interleave(nc.vector.tensor_copy, theta_raw[:, :, h * P : (h + 1) * P], P, "theta_bf%d" % h) for h in range(2)]
+        theta_mx = [quantize(halves[h], P, "theta%d" % h) for h in range(2)]
+        gain = [psum.tile([P, Q], F32, name="gain%d" % t) for t in range(2)]
+        gain = gain + [zpsum.tile([P, Q], F32, name="gain%d" % t, tag="z") for t in range(2, I_TILES)]
+        for h in range(2):
+            for t in range(I_TILES):
+                cols = slice(t * P, (t + 1) * P)
+                nc.tensor.matmul_mx(
+                    out=gain[t][:, h * P : (h + 1) * P],
+                    lhsT=cand_q[:, cols].bitcast(FP8X4),
+                    lhsT_scale=cand_s[:, cols],
+                    rhs=theta_mx[h][0][:].bitcast(FP8X4),
+                    rhs_scale=theta_mx[h][1][:],
+                    start=True,
+                    stop=True,
+                )
 
         for t in range(I_TILES):
             res = keep.tile([P, Q], F32, name="res%d" % t)
             nc.vector.scalar_tensor_tensor(
                 out=res[:],
                 in0=bold_row[:],
-                scalar=widths[t][:],
-                in1=gain[t // 2][:, t % 2, :],
+                scalar=widths[t],
+                in1=gain[t][:],
                 op0=ALU.mult,
                 op1=ALU.add,
             )

@@ -18,9 +18,14 @@ ACT = mybir.ActivationFunctionType
 
 P = 128
 PACK = 4
+QUADRANTS = 4
 K_TILES = K // P
 I_TILES = I // P
+Q_HALVES = Q // P
 OFFS_COLS = P // 16
+CLEAR_SPLIT = 320
+INV_TILES_ON_VECTOR = 2
+EARLY_TILES = 2
 
 
 def tile_attend_confidencebounds_kernel(tc, cand_words, cand_scales, theta, inv, crow, bold, offs, out):
@@ -28,81 +33,84 @@ def tile_attend_confidencebounds_kernel(tc, cand_words, cand_scales, theta, inv,
     with ExitStack() as ctx:
         keep = ctx.enter_context(tc.tile_pool(name="keep", bufs=1))
         psum = ctx.enter_context(tc.psum_pool(name="psum", bufs=1))
-        zpsum = ctx.enter_context(tc.psum_pool(name="zpsum", bufs=2))
+        ring = ctx.enter_context(tc.psum_pool(name="ring", bufs=2))
 
         offsets = keep.tile([P, I // 16], U16, name="offsets")
         inv_raw = keep.tile([P, PACK, K], F32, name="inv_raw")
-        words = keep.tile([P, T], U32, name="words", align_bytes=64)
-        scales = keep.tile([P, T], U8, name="scales", align_bytes=64)
+        store_words = keep.tile([P, T], U32, name="store_words", align_bytes=64)
+        store_scales = keep.tile([P, T], U8, name="store_scales", align_bytes=64)
         theta_raw = keep.tile([P, PACK, Q], F32, name="theta_raw")
         crow_sb = [keep.tile([P, T], F32, name="crow%d" % j) for j in range(K_TILES)]
         bold_col = keep.tile([P, 2], F32, name="bold_col")
 
-        scale_words = scales[:].bitcast(I32)
-        nc.vector.memset(scale_words[:, 0:320], 0)
-        nc.gpsimd.memset(scale_words[:, 320:], 0)
+        scales_i32 = store_scales[:].bitcast(I32)
+        nc.vector.memset(scales_i32[:, 0:CLEAR_SPLIT], 0)
+        nc.gpsimd.memset(scales_i32[:, CLEAR_SPLIT:], 0)
+
+        words_hbm = cand_words[0].rearrange("p n t -> p (n t)").bitcast(I32)
+        words_i32 = store_words[:].bitcast(I32)
+        nc.sync.dma_start(out=words_i32[:, 0 : T // 2], in_=words_hbm[:, 0 : T // 2])
         nc.sync.dma_start(offsets[:], offs)
-        nc.sync.dma_start(out=inv_raw[:], in_=inv.rearrange("(p j) w -> p j w", j=PACK))
-        nc.sync.dma_start(out=bold_col[:], in_=bold[0].rearrange("(p c) -> p c", c=2))
-        for g in range(4):
+        nc.gpsimd.dma_start(out=bold_col[:], in_=bold[0].rearrange("(p c) -> p c", c=2))
+        nc.sync.dma_start(out=words_i32[:, T // 2 :], in_=words_hbm[:, T // 2 :])
+        for g in range(QUADRANTS):
             nc.sync.dma_start(
-                out=scales[32 * g : 32 * g + 4, :].bitcast(I32),
+                out=scales_i32[32 * g : 32 * g + 4, :],
                 in_=cand_scales[0, 4 * g : 4 * g + 4, :].bitcast(I32),
             )
-        nc.sync.dma_start(out=words[:].bitcast(I32), in_=cand_words[0].rearrange("p n t -> p (n t)").bitcast(I32))
-        nc.sync.dma_start(out=crow_sb[0][:], in_=crow[0:P, :])
-        for j in range(1, K_TILES):
+        nc.sync.dma_start(out=inv_raw[:], in_=inv.rearrange("(p t) w -> p t w", t=PACK))
+        for j in range(K_TILES):
             nc.sync.dma_start(out=crow_sb[j][:], in_=crow[j * P : (j + 1) * P, :])
-        nc.sync.dma_start(out=theta_raw[:], in_=theta.rearrange("(p j) w -> p j w", j=PACK))
+        nc.sync.dma_start(out=theta_raw[:], in_=theta.rearrange("(p t) w -> p t w", t=PACK))
 
         ident = keep.tile([P, P], F32, name="ident")
         make_identity(nc, ident[:])
-        warm = keep.tile([P, 1], F32, name="warm")
-        one = keep.tile([P, 1], F32, name="one")
-        nc.vector.memset(one[:], 1.0)
-        nc.scalar.activation(out=warm[:], in_=one[:], func=ACT.Sqrt)
 
-        cand_s = keep.tile([P, I], U8, name="cand_s", align_bytes=64)
-        nc.vector.tensor_copy(cand_s[:], scales[:].indirect(offsets[:]))
+        inv_k = keep.tile([P, 1], F32, name="inv_k")
+        nc.vector.memset(inv_k[:], 1.0 / K)
+        root_inv_k = keep.tile([P, 1], F32, name="root_inv_k")
+        nc.scalar.activation(out=root_inv_k[:], in_=inv_k[:], func=ACT.Sqrt)
 
-        def interleave(copy, raw, width, name):
-            grouped = keep.tile([P, width, PACK], BF16, name=name, align_bytes=64)
+        cand_codes = keep.tile([P, I], U32, name="cand_codes", align_bytes=64)
+        nc.vector.tensor_copy(cand_codes[:], store_words[:].indirect(offsets[:]))
+        cand_plane = keep.tile([P, I], U8, name="cand_plane", align_bytes=64)
+        nc.vector.tensor_copy(cand_plane[:], store_scales[:].indirect(offsets[:]))
+
+        def interleave(copy, raw, name):
+            grouped = keep.tile([P, P, PACK], BF16, name=name, align_bytes=64)
             copy(
                 out=grouped[:].rearrange("p (c i) t -> p c t i", i=4),
                 in_=raw.rearrange("p t (c i) -> p c t i", i=4),
             )
             return grouped
 
-        def quantize(grouped, width, name):
-            codes = keep.tile([P, width], U32, name=name + "_codes", align_bytes=64)
-            plane = keep.tile([P, width], U8, name=name + "_scales", align_bytes=64)
+        def quantize(grouped, name):
+            codes = keep.tile([P, P], U32, name=name + "_codes", align_bytes=64)
+            plane = keep.tile([P, P], U8, name=name + "_plane", align_bytes=64)
             nc.vector.quantize_mx(
                 out=codes[:].bitcast(FP8X4), scales=plane[:], in_=grouped[:].rearrange("p w t -> p (w t)")
             )
             return codes, plane
 
-        inv_bf = interleave(nc.vector.tensor_copy, inv_raw[:], K, "inv_bf")
-        inv_q, inv_s = quantize(inv_bf, K, "inv")
-
-        cand_q = keep.tile([P, I], U32, name="cand_q", align_bytes=64)
-        nc.vector.tensor_copy(cand_q[:], words[:].indirect(offsets[:]))
-
-        bold_ps = zpsum.tile([P, 2, P], F32, name="bold_ps", tag="z")
-        for c in range(2):
-            nc.tensor.transpose(bold_ps[:, c, :], bold_col[:, c : c + 1].to_broadcast([P, P]), ident[:])
-        bold_row = keep.tile([P, Q], F32, name="bold_row")
-        nc.scalar.copy(out=bold_row[:].rearrange("p (n c) -> p n c", c=2), in_=bold_ps[:].rearrange("p c n -> p n c"))
+        inv_bf = [
+            interleave(
+                nc.vector.tensor_copy if j < INV_TILES_ON_VECTOR else nc.scalar.copy,
+                inv_raw[:, :, j * P : (j + 1) * P],
+                "inv_bf%d" % j,
+            )
+            for j in range(K_TILES)
+        ]
+        inv_mx = [quantize(inv_bf[j], "inv%d" % j) for j in range(K_TILES)]
 
         z_sb = []
         for j in range(K_TILES):
-            cols = slice(j * P, (j + 1) * P)
-            z_ps = zpsum.tile([P, I], F32, name="z_ps%d" % j, tag="z")
+            z_ps = ring.tile([P, I], F32, name="z_ps%d" % j, tag="ring")
             nc.tensor.matmul_mx(
                 out=z_ps[:],
-                lhsT=inv_q[:, cols].bitcast(FP8X4),
-                lhsT_scale=inv_s[:, cols],
-                rhs=cand_q[:].bitcast(FP8X4),
-                rhs_scale=cand_s[:],
+                lhsT=inv_mx[j][0][:].bitcast(FP8X4),
+                lhsT_scale=inv_mx[j][1][:],
+                rhs=cand_codes[:].bitcast(FP8X4),
+                rhs_scale=cand_plane[:],
                 start=True,
                 stop=True,
             )
@@ -110,7 +118,18 @@ def tile_attend_confidencebounds_kernel(tc, cand_words, cand_scales, theta, inv,
             nc.scalar.copy(out=z_tile[:], in_=z_ps[:])
             z_sb.append(z_tile)
 
-        form = [psum.tile([P, P], F32, name="form%d" % t) for t in range(I_TILES)]
+        bold_ps = ring.tile([P, 2, P], F32, name="bold_ps", tag="ring")
+        for c in range(2):
+            nc.tensor.transpose(bold_ps[:, c, :], bold_col[:, c : c + 1].to_broadcast([P, P]), ident[:])
+        bold_row = keep.tile([P, Q], F32, name="bold_row")
+        nc.scalar.activation(
+            out=bold_row[:].rearrange("p (n c) -> p n c", c=2),
+            in_=bold_ps[:].rearrange("p c n -> p n c"),
+            func=ACT.Copy,
+            scale=root_inv_k[:],
+        )
+
+        form = [psum.tile([P, P], F32, name="form%d" % t, tag="form%d" % t) for t in range(I_TILES)]
 
         def gather_times_z(j, t0, t1):
             prod = keep.tile([P, (t1 - t0) * P], F32, name="prod%d_%d" % (j, t0))
@@ -133,44 +152,60 @@ def tile_attend_confidencebounds_kernel(tc, cand_words, cand_scales, theta, inv,
         for j in range(K_TILES - 1):
             gather_times_z(j, 0, I_TILES)
 
-        widths = []
+        roots = []
         for pair in range(I_TILES // 2):
             gather_times_z(K_TILES - 1, 2 * pair, 2 * pair + 2)
             total = keep.tile([P, 2], F32, name="total%d" % pair)
             for u in range(2):
                 spill = keep.tile([P, P], F32, name="spill%d_%d" % (pair, u))
-                nc.scalar.activation(out=spill[:], in_=form[2 * pair + u][:], func=ACT.Copy, accum_out=total[:, u : u + 1])
+                nc.scalar.activation(
+                    out=spill[:], in_=form[2 * pair + u][:], func=ACT.Copy, accum_out=total[:, u : u + 1]
+                )
             size = keep.tile([P, 2], F32, name="size%d" % pair)
             nc.scalar.activation(out=size[:], in_=total[:], func=ACT.Abs)
-            width = keep.tile([P, 2], F32, name="width%d" % pair)
-            nc.scalar.activation(out=width[:], in_=size[:], func=ACT.Sqrt, scale=1.0 / K, bias=0.01)
-            widths.extend([width[:, 0:1], width[:, 1:2]])
+            root = keep.tile([P, 2], F32, name="root%d" % pair)
+            nc.scalar.activation(out=root[:], in_=size[:], func=ACT.Sqrt, bias=0.01 * K)
+            roots.extend([root[:, 0:1], root[:, 1:2]])
 
-        halves = [interleave(nc.vector.tensor_copy, theta_raw[:, :, h * P : (h + 1) * P], P, "theta_bf%d" % h) for h in range(2)]
-        theta_mx = [quantize(halves[h], P, "theta%d" % h) for h in range(2)]
-        gain = [psum.tile([P, Q], F32, name="gain%d" % t) for t in range(2)]
-        gain = gain + [zpsum.tile([P, Q], F32, name="gain%d" % t, tag="z") for t in range(2, I_TILES)]
-        for h in range(2):
+        theta_bf = [
+            interleave(nc.vector.tensor_copy, theta_raw[:, :, h * P : (h + 1) * P], "theta_bf%d" % h)
+            for h in range(Q_HALVES)
+        ]
+        theta_mx = [quantize(theta_bf[h], "theta%d" % h) for h in range(Q_HALVES)]
+
+        first = [psum.tile([P, P], F32, name="first%d" % t) for t in range(EARLY_TILES)]
+        second = [psum.tile([P, P], F32, name="second%d" % t, tag="form%d" % t) for t in range(EARLY_TILES)]
+        whole = [ring.tile([P, Q], F32, name="whole%d" % t, tag="ring") for t in range(EARLY_TILES, I_TILES)]
+        gain = [[first[t][:], second[t][:]] for t in range(EARLY_TILES)]
+        gain = gain + [[bank[:, 0:P], bank[:, P:Q]] for bank in whole]
+        for h in range(Q_HALVES):
             for t in range(I_TILES):
                 cols = slice(t * P, (t + 1) * P)
                 nc.tensor.matmul_mx(
-                    out=gain[t][:, h * P : (h + 1) * P],
-                    lhsT=cand_q[:, cols].bitcast(FP8X4),
-                    lhsT_scale=cand_s[:, cols],
+                    out=gain[t][h],
+                    lhsT=cand_codes[:, cols].bitcast(FP8X4),
+                    lhsT_scale=cand_plane[:, cols],
                     rhs=theta_mx[h][0][:].bitcast(FP8X4),
                     rhs_scale=theta_mx[h][1][:],
                     start=True,
                     stop=True,
                 )
 
-        for t in range(I_TILES):
-            res = keep.tile([P, Q], F32, name="res%d" % t)
+        res = [keep.tile([P, Q], F32, name="res%d" % t) for t in range(I_TILES)]
+
+        def finish(t, users, gain_ps):
             nc.vector.scalar_tensor_tensor(
-                out=res[:],
-                in0=bold_row[:],
-                scalar=widths[t],
-                in1=gain[t][:],
-                op0=ALU.mult,
-                op1=ALU.add,
+                out=res[t][:, users], in0=bold_row[:, users], scalar=roots[t], in1=gain_ps, op0=ALU.mult, op1=ALU.add
             )
-            nc.sync.dma_start(out=out[t * P : (t + 1) * P, :], in_=res[:])
+
+        def store(t):
+            nc.sync.dma_start(out=out[t * P : (t + 1) * P, :], in_=res[t][:])
+
+        for t in range(EARLY_TILES):
+            finish(t, slice(0, P), gain[t][0])
+        for t in range(EARLY_TILES):
+            finish(t, slice(P, Q), gain[t][1])
+            store(t)
+        for t in range(EARLY_TILES, I_TILES):
+            finish(t, slice(0, Q), whole[t - EARLY_TILES][:])
+            store(t)

from contextlib import ExitStack

import concourse.mybir as mybir
from concourse.masks import make_identity

D, K, T, I, Q = 512, 512, 2048, 512, 256
FLOPS = 2 * D * I * (Q + K)

F32 = mybir.dt.float32
BF16 = mybir.dt.bfloat16
I32 = mybir.dt.int32
U32 = mybir.dt.uint32
U16 = mybir.dt.uint16
U8 = mybir.dt.uint8
FP8X4 = mybir.dt.float8_e4m3fn_x4
ALU = mybir.AluOpType
ACT = mybir.ActivationFunctionType

P = 128
PACK = 4
QUADRANTS = 4
K_TILES = K // P
I_TILES = I // P
Q_HALVES = Q // P
OFFS_COLS = P // 16
CLEAR_SPLIT = 320
INV_TILES_ON_VECTOR = 2
EARLY_TILES = 2


def tile_attend_confidencebounds_kernel(tc, cand_words, cand_scales, theta, inv, crow, bold, offs, out):
    nc = tc.nc
    with ExitStack() as ctx:
        keep = ctx.enter_context(tc.tile_pool(name="keep", bufs=1))
        psum = ctx.enter_context(tc.psum_pool(name="psum", bufs=1))
        ring = ctx.enter_context(tc.psum_pool(name="ring", bufs=2))

        offsets = keep.tile([P, I // 16], U16, name="offsets")
        inv_raw = keep.tile([P, PACK, K], F32, name="inv_raw")
        store_words = keep.tile([P, T], U32, name="store_words", align_bytes=64)
        store_scales = keep.tile([P, T], U8, name="store_scales", align_bytes=64)
        theta_raw = keep.tile([P, PACK, Q], F32, name="theta_raw")
        crow_sb = [keep.tile([P, T], F32, name="crow%d" % j) for j in range(K_TILES)]
        bold_col = keep.tile([P, 2], F32, name="bold_col")

        scales_i32 = store_scales[:].bitcast(I32)
        nc.vector.memset(scales_i32[:, 0:CLEAR_SPLIT], 0)
        nc.gpsimd.memset(scales_i32[:, CLEAR_SPLIT:], 0)

        words_hbm = cand_words[0].rearrange("p n t -> p (n t)").bitcast(I32)
        words_i32 = store_words[:].bitcast(I32)
        nc.sync.dma_start(out=words_i32[:, 0 : T // 2], in_=words_hbm[:, 0 : T // 2])
        nc.sync.dma_start(offsets[:], offs)
        nc.gpsimd.dma_start(out=bold_col[:], in_=bold[0].rearrange("(p c) -> p c", c=2))
        nc.sync.dma_start(out=words_i32[:, T // 2 :], in_=words_hbm[:, T // 2 :])
        for g in range(QUADRANTS):
            nc.sync.dma_start(
                out=scales_i32[32 * g : 32 * g + 4, :],
                in_=cand_scales[0, 4 * g : 4 * g + 4, :].bitcast(I32),
            )
        nc.sync.dma_start(out=inv_raw[:], in_=inv.rearrange("(p t) w -> p t w", t=PACK))
        for j in range(K_TILES):
            nc.sync.dma_start(out=crow_sb[j][:], in_=crow[j * P : (j + 1) * P, :])
        nc.sync.dma_start(out=theta_raw[:], in_=theta.rearrange("(p t) w -> p t w", t=PACK))

        ident = keep.tile([P, P], F32, name="ident")
        make_identity(nc, ident[:])

        inv_k = keep.tile([P, 1], F32, name="inv_k")
        nc.vector.memset(inv_k[:], 1.0 / K)
        root_inv_k = keep.tile([P, 1], F32, name="root_inv_k")
        nc.scalar.activation(out=root_inv_k[:], in_=inv_k[:], func=ACT.Sqrt)

        cand_codes = keep.tile([P, I], U32, name="cand_codes", align_bytes=64)
        nc.vector.tensor_copy(cand_codes[:], store_words[:].indirect(offsets[:]))
        cand_plane = keep.tile([P, I], U8, name="cand_plane", align_bytes=64)
        nc.vector.tensor_copy(cand_plane[:], store_scales[:].indirect(offsets[:]))

        def interleave(copy, raw, name):
            grouped = keep.tile([P, P, PACK], BF16, name=name, align_bytes=64)
            copy(
                out=grouped[:].rearrange("p (c i) t -> p c t i", i=4),
                in_=raw.rearrange("p t (c i) -> p c t i", i=4),
            )
            return grouped

        def quantize(grouped, name):
            codes = keep.tile([P, P], U32, name=name + "_codes", align_bytes=64)
            plane = keep.tile([P, P], U8, name=name + "_plane", align_bytes=64)
            nc.vector.quantize_mx(
                out=codes[:].bitcast(FP8X4), scales=plane[:], in_=grouped[:].rearrange("p w t -> p (w t)")
            )
            return codes, plane

        inv_bf = [
            interleave(
                nc.vector.tensor_copy if j < INV_TILES_ON_VECTOR else nc.scalar.copy,
                inv_raw[:, :, j * P : (j + 1) * P],
                "inv_bf%d" % j,
            )
            for j in range(K_TILES)
        ]
        inv_mx = [quantize(inv_bf[j], "inv%d" % j) for j in range(K_TILES)]

        z_sb = []
        for j in range(K_TILES):
            z_ps = ring.tile([P, I], F32, name="z_ps%d" % j, tag="ring")
            nc.tensor.matmul_mx(
                out=z_ps[:],
                lhsT=inv_mx[j][0][:].bitcast(FP8X4),
                lhsT_scale=inv_mx[j][1][:],
                rhs=cand_codes[:].bitcast(FP8X4),
                rhs_scale=cand_plane[:],
                start=True,
                stop=True,
            )
            z_tile = keep.tile([P, I], F32, name="z_sb%d" % j)
            nc.scalar.copy(out=z_tile[:], in_=z_ps[:])
            z_sb.append(z_tile)

        bold_ps = ring.tile([P, 2, P], F32, name="bold_ps", tag="ring")
        for c in range(2):
            nc.tensor.transpose(bold_ps[:, c, :], bold_col[:, c : c + 1].to_broadcast([P, P]), ident[:])
        bold_row = keep.tile([P, Q], F32, name="bold_row")
        nc.scalar.activation(
            out=bold_row[:].rearrange("p (n c) -> p n c", c=2),
            in_=bold_ps[:].rearrange("p c n -> p n c"),
            func=ACT.Copy,
            scale=root_inv_k[:],
        )

        form = [psum.tile([P, P], F32, name="form%d" % t, tag="form%d" % t) for t in range(I_TILES)]

        def gather_times_z(j, t0, t1):
            prod = keep.tile([P, (t1 - t0) * P], F32, name="prod%d_%d" % (j, t0))
            nc.vector.tensor_tensor(
                prod[:],
                crow_sb[j][:].indirect(offsets[:, t0 * OFFS_COLS : t1 * OFFS_COLS]),
                z_sb[j][:, t0 * P : t1 * P],
                ALU.mult,
            )
            for t in range(t0, t1):
                nc.tensor.matmul(
                    form[t][:],
                    lhsT=prod[:, (t - t0) * P : (t - t0 + 1) * P],
                    rhs=ident[:],
                    is_transpose=True,
                    start=(j == 0),
                    stop=(j == K_TILES - 1),
                )

        for j in range(K_TILES - 1):
            gather_times_z(j, 0, I_TILES)

        roots = []
        for pair in range(I_TILES // 2):
            gather_times_z(K_TILES - 1, 2 * pair, 2 * pair + 2)
            total = keep.tile([P, 2], F32, name="total%d" % pair)
            for u in range(2):
                spill = keep.tile([P, P], F32, name="spill%d_%d" % (pair, u))
                nc.scalar.activation(
                    out=spill[:], in_=form[2 * pair + u][:], func=ACT.Copy, accum_out=total[:, u : u + 1]
                )
            size = keep.tile([P, 2], F32, name="size%d" % pair)
            nc.scalar.activation(out=size[:], in_=total[:], func=ACT.Abs)
            root = keep.tile([P, 2], F32, name="root%d" % pair)
            nc.scalar.activation(out=root[:], in_=size[:], func=ACT.Sqrt, bias=0.01 * K)
            roots.extend([root[:, 0:1], root[:, 1:2]])

        theta_bf = [
            interleave(nc.vector.tensor_copy, theta_raw[:, :, h * P : (h + 1) * P], "theta_bf%d" % h)
            for h in range(Q_HALVES)
        ]
        theta_mx = [quantize(theta_bf[h], "theta%d" % h) for h in range(Q_HALVES)]

        first = [psum.tile([P, P], F32, name="first%d" % t) for t in range(EARLY_TILES)]
        second = [psum.tile([P, P], F32, name="second%d" % t, tag="form%d" % t) for t in range(EARLY_TILES)]
        whole = [ring.tile([P, Q], F32, name="whole%d" % t, tag="ring") for t in range(EARLY_TILES, I_TILES)]
        gain = [[first[t][:], second[t][:]] for t in range(EARLY_TILES)]
        gain = gain + [[bank[:, 0:P], bank[:, P:Q]] for bank in whole]
        for h in range(Q_HALVES):
            for t in range(I_TILES):
                cols = slice(t * P, (t + 1) * P)
                nc.tensor.matmul_mx(
                    out=gain[t][h],
                    lhsT=cand_codes[:, cols].bitcast(FP8X4),
                    lhsT_scale=cand_plane[:, cols],
                    rhs=theta_mx[h][0][:].bitcast(FP8X4),
                    rhs_scale=theta_mx[h][1][:],
                    start=True,
                    stop=True,
                )

        res = [keep.tile([P, Q], F32, name="res%d" % t) for t in range(I_TILES)]

        def finish(t, users, gain_ps):
            nc.vector.scalar_tensor_tensor(
                out=res[t][:, users], in0=bold_row[:, users], scalar=roots[t], in1=gain_ps, op0=ALU.mult, op1=ALU.add
            )

        def store(t):
            nc.sync.dma_start(out=out[t * P : (t + 1) * P, :], in_=res[t][:])

        for t in range(EARLY_TILES):
            finish(t, slice(0, P), gain[t][0])
        for t in range(EARLY_TILES):
            finish(t, slice(P, Q), gain[t][1])
            store(t)
        for t in range(EARLY_TILES, I_TILES):
            finish(t, slice(0, Q), whole[t - EARLY_TILES][:])
            store(t)
